import numpy as np
import ml_dtypes


def mxq(x, axis, fmt="e4m3"):
    dtype, down = {"e4m3": (ml_dtypes.float8_e4m3fn, 7), "e5m2": (ml_dtypes.float8_e5m2, 14)}[fmt]
    v = np.moveaxis(np.asarray(x, np.float32).astype(ml_dtypes.bfloat16).astype(np.float64), axis, -1)
    blocks = v.reshape(v.shape[:-1] + (-1, 32))
    amax = np.abs(blocks).max(-1, keepdims=True)
    byte = np.maximum(np.where(amax > 0, np.frexp(amax)[1] - 1 + 127, 0) - down, 1)
    scale = np.exp2(byte - 127.0)
    codes = (blocks / scale).astype(np.float32).astype(dtype).astype(np.float64)
    return np.moveaxis((codes * scale).reshape(v.shape), -1, axis)


WIDE = False


def mx_kscale(k):
    if not WIDE:
        return np.ones(k)
    levels = np.array([10, -10, 5, -5, 0])
    if k % 512:
        return np.exp2(np.random.permutation(np.resize(levels, k // 32))).repeat(32)
    a = np.empty((k // 512, 16))
    for p in range(k // 512):
        a[p, :8] = np.random.permutation(np.resize(levels, 8))
        for g in range(8):
            far = levels[np.abs(levels - a[p, g]) >= 10]
            a[p, g + 8] = far[np.random.randint(len(far))]
    return np.exp2(a.ravel()).repeat(32)


def f64(x):
    return np.asarray(x).astype(np.float64)


def striped(idx):
    return np.tile(np.asarray(idx).reshape(-1, 16).T, (8, 1)).astype(np.uint16)


def unstriped(offs):
    return offs[:16].T.reshape(-1).astype(np.int64)


E2M1 = np.array([0.0, 0.5, 1.0, 1.5, 2.0, 3.0, 4.0, 6.0, -0.0, -0.5, -1.0, -1.5, -2.0, -3.0, -4.0, -6.0])


def pack_weight(w, fmt):
    k, n = w.shape
    w = f64(np.asarray(w, np.float32).astype(ml_dtypes.bfloat16)).reshape(k // 32, 32, n)
    amax = np.abs(w).max(1)
    if fmt == "e4m3":
        byte = np.frexp(amax)[1] - 1 + 127 - 7
    else:
        mant, ex = np.frexp(amax / 6.0)
        byte = np.where(mant > 0.5, ex, ex - 1) + 127
    byte = np.clip(np.where(amax > 0, byte, 1), 1, 254)
    scaled = (w * np.exp2(127.0 - byte)[:, None, :]).reshape(k, n).astype(np.float32)
    by_word = np.ascontiguousarray(scaled.reshape(k // 512, 128, 4, n).transpose(0, 1, 3, 2))
    if fmt == "e4m3":
        words = by_word.astype(ml_dtypes.float8_e4m3fn).view(np.uint8)
    else:
        c = by_word.astype(ml_dtypes.float4_e2m1fn).view(np.uint8) & 0xF
        words = (c[..., 0::2] | (c[..., 1::2] << 4)).reshape(k // 512, 128, 2 * n)
    return np.ascontiguousarray(words), np.ascontiguousarray(byte.astype(np.uint8).reshape(k // 512, 16, n))


def unpack_weight(words, scales, fmt):
    g, _, n = scales.shape
    words = np.ascontiguousarray(words).reshape(g, 128, n, -1)
    if fmt == "e4m3":
        vals = words.view(ml_dtypes.float8_e4m3fn).astype(np.float64)
    else:
        nib = np.empty((g, 128, n, 4), np.uint8)
        nib[..., 0::2] = words & 0xF
        nib[..., 1::2] = words >> 4
        vals = E2M1[nib]
    vals = vals * np.repeat(np.exp2(scales.astype(np.float64) - 127.0), 8, axis=1)[..., None]
    return vals.transpose(0, 1, 3, 2).reshape(g * 512, n)


def softplus(v):
    return np.log(1.0 + np.exp(v))


def sigmoid(v):
    return 1.0 / (1.0 + np.exp(-v))


D, E, T, I, G, U, Q = 512, 512, 4096, 1024, 64, 512, 128


def setup_inputs():
    n = np.random.standard_normal
    idx = np.random.permutation(T)[:I]
    idx2 = np.random.permutation(U)[:G]
    fd = mx_kscale(D)
    fe = mx_kscale(E)
    keysp = pack_weight(n((D, T)) / fd[:, None], "e2m1")
    valsp = pack_weight(n((E, T)) / fe[:, None], "e2m1")
    return {
        "query": (n((D, Q)) * 1.0 / np.sqrt(D) * fd[:, None]).astype(np.float32),
        "keys_words": keysp[0],
        "keys_scales": keysp[1],
        "ptab": (n((Q, U)) * 0.5).astype(np.float32),
        "reserve": (np.random.uniform(50.0, 200.0, (Q, 1))).astype(np.float32),
        "gout": (n((E, Q)) * 1 / np.sqrt(E) * fe[:, None]).astype(np.float32),
        "vals_words": valsp[0],
        "vals_scales": valsp[1],
        "lam": (np.random.uniform(0.5, 1.5, (Q, 1))).astype(np.float32),
        "old": (0.5 * n((Q, U))).astype(np.float32),
        "offs": striped(idx),
        "offs2": striped(idx2),
    }


def reference(query, keys_words, keys_scales, ptab, reserve, gout, vals_words, vals_scales, lam, old, offs, offs2):
    idx = unstriped(offs)
    idx2 = unstriped(offs2)
    keysu = unpack_weight(keys_words, keys_scales, "e2m1")
    valsu = unpack_weight(vals_words, vals_scales, "e2m1")
    queryq = mxq(f64(query), 0, "e4m3")
    keysidxg = keysu[:, idx]
    a = queryq.T @ keysidxg
    tp = f64(ptab)[:, idx2] * f64(lam)
    tr1 = np.repeat(tp, I // G, axis=1)
    p = softplus(a - tr1)
    z = np.sum(p, axis=1, keepdims=True) + f64(reserve)
    goutq = mxq(f64(gout), 0, "e4m3")
    valsidxg = valsu[:, idx]
    c0 = goutq.T @ valsidxg
    dz = np.sum(p * c0, axis=1, keepdims=True) / np.square(z) * (-1.0)
    dp = 1.0 / z * c0 + dz
    dtr1 = dp * sigmoid(a - tr1) * (-1.0)
    dtp = dtr1.reshape(Q, G, I // G).sum(axis=2)
    gs = dtp * f64(lam) * 64.0
    gf = np.zeros((Q, U))
    gf[:, idx2] = gs
    y = f64(old) + gf
    return y

@@ -1,0 +1,200 @@
+from contextlib import ExitStack
+
+import concourse.mybir as mybir
+
+D, T, I, G, U, Q = 512, 4096, 1024, 64, 512, 128
+FLOPS = 2 * 2 * D * I * Q
+
+F32 = mybir.dt.float32
+BF16 = mybir.dt.bfloat16
+I32 = mybir.dt.int32
+U32 = mybir.dt.uint32
+U16 = mybir.dt.uint16
+U8 = mybir.dt.uint8
+FP8X4 = mybir.dt.float8_e4m3fn_x4
+FP4X4 = mybir.dt.float4_e2m1fn_x4
+ALU = mybir.AluOpType
+ACT = mybir.ActivationFunctionType
+
+P = 128
+PACK = 4
+PAGE = I // G
+HALF = 512
+HALVES = I // HALF
+PAGES_H = HALF // PAGE
+LOG_FLOOR = 2.0 ** -60
+
+
+def tile_attend_bpagefloor_kernel(tc, query, keys_words, keys_scales, ptab, reserve, gout, vals_words,
+                                   vals_scales, lam, old, offs, offs2, out):
+    nc = tc.nc
+    with ExitStack() as ctx:
+        lists = ctx.enter_context(tc.tile_pool(name="lists", bufs=1))
+        keep = ctx.enter_context(tc.tile_pool(name="keep", bufs=1))
+        shared = ctx.enter_context(tc.tile_pool(name="shared", bufs=1))
+        psum = ctx.enter_context(tc.psum_pool(name="psum", bufs=1))
+
+        slots = lists.tile([P, I // 16], U16, name="slots")
+        pages = lists.tile([P, G // 16], U16, name="pages")
+
+        ones_at = 8192
+        qraw_at = 16384
+        qbf_at = 32768
+        floors_at = 40960
+        k_scales = keep.tile([P, T], U8, name="k_scales")
+        nc.vector.memset(k_scales[:].bitcast(I32), 0)
+        ones = shared.tile([P, P], F32, name="ones", offset=ones_at)
+        nc.vector.memset(ones[:], 1.0)
+        ident = keep.tile([P, P], F32, name="ident")
+        nc.gpsimd.affine_select(out=ident[:], in_=ones[:], compare_op=ALU.is_equal, fill=0.0, base=0,
+                                pattern=[[-1, P]], channel_multiplier=1)
+        v_scales = shared.tile([P, T], U8, name="v_scales", offset=ones_at + 480)
+        nc.vector.memset(v_scales[:].bitcast(I32), 0)
+        grad = keep.tile([P, U], F32, name="grad")
+        nc.vector.memset(grad[:], 0.0)
+
+        def load_scales(tile, scales):
+            rows = scales[0].rearrange("(quad r) c -> r quad c", r=4)
+            for r in range(4):
+                nc.sync.dma_start(out=tile[r:P:32, :].bitcast(I32), in_=rows[r].bitcast(I32))
+
+        def interleave(raw, grouped):
+            nc.scalar.copy(out=grouped[:].rearrange("p (c i) t -> p c t i", i=4),
+                           in_=raw[:].rearrange("p t (c i) -> p c t i", i=4))
+
+        def quantize(grouped, name):
+            codes = keep.tile([P, Q], U32, name=name + "_codes", align_bytes=64)
+            scales = keep.tile([P, Q], U8, name=name + "_scales", align_bytes=64)
+            nc.vector.quantize_mx(out=codes[:].bitcast(FP8X4), scales=scales[:],
+                                  in_=grouped[:].rearrange("p w t -> p (w t)"))
+            return codes, scales
+
+        nc.sync.dma_start(slots[:], offs)
+        q_raw = shared.tile([P, PACK, Q], F32, name="q_raw", offset=qraw_at)
+        nc.sync.dma_start(out=q_raw[:], in_=query.rearrange("(p t) w -> p t w", t=PACK))
+        nc.sync.dma_start(pages[:], offs2)
+        load_scales(k_scales, keys_scales)
+        k_words = shared.tile([P, T], U16, name="k_words", offset=ones_at + 32 - 2 * T)
+        nc.sync.dma_start(out=k_words[:].bitcast(I32), in_=keys_words[0].bitcast(I32))
+
+        q_bf = shared.tile([P, Q, PACK], BF16, name="q_bf", offset=qbf_at, align_bytes=64)
+        interleave(q_raw, q_bf)
+
+        table = shared.tile([P, U], F32, name="table", offset=qraw_at + 2016)
+        nc.sync.dma_start(out=table[:], in_=ptab)
+        lam_sb = shared.tile([P, 1], F32, name="lam_sb", offset=ones_at + 64)
+        nc.sync.dma_start(out=lam_sb[:], in_=lam)
+        g_raw = shared.tile([P, PACK, Q], F32, name="g_raw", offset=qraw_at + 32 - 2048)
+        nc.sync.dma_start(out=g_raw[:], in_=gout.rearrange("(p t) w -> p t w", t=PACK))
+        load_scales(v_scales, vals_scales)
+
+        ks = keep.tile([P, I], U8, name="ks", align_bytes=64)
+        nc.vector.tensor_copy(ks[:], k_scales[:].indirect(slots[:]))
+        q_codes, q_scales = quantize(q_bf, "q")
+
+        v_words = shared.tile([P, T], U16, name="v_words", offset=qbf_at + 32 - 2 * T)
+        nc.sync.dma_start(out=v_words[:].bitcast(I32), in_=vals_words[0].bitcast(I32))
+        res_sb = shared.tile([P, 1], F32, name="res_sb", offset=ones_at + 96)
+        nc.sync.dma_start(out=res_sb[:], in_=reserve)
+        old_sb = shared.tile([P, U], F32, name="old_sb", offset=qbf_at + 992)
+        nc.sync.dma_start(out=old_sb[:], in_=old)
+
+        g_bf = keep.tile([P, Q, PACK], BF16, name="g_bf", align_bytes=64)
+        interleave(g_raw, g_bf)
+        factor = keep.tile([P, 1], F32, name="factor")
+        nc.scalar.activation(out=factor[:], in_=lam_sb[:], func=ACT.Copy, scale=-64.0)
+
+        def product(words, gathered_scales, codes, scales, name):
+            banks = []
+            for h in range(HALVES):
+                picked = keep.tile([P, HALF], U16, name="%s_picked%d" % (name, h), align_bytes=64)
+                cols = slice(h * HALF // 16, (h + 1) * HALF // 16)
+                nc.vector.tensor_copy(picked[:], words[:].indirect(slots[:, cols]))
+                bank = psum.tile([P, HALF], F32, name="%s_bank%d" % (name, h))
+                nc.tensor.matmul_mx(out=bank[:], lhsT=codes[:].bitcast(FP8X4), lhsT_scale=scales[:],
+                                    rhs=picked[:].bitcast(FP4X4),
+                                    rhs_scale=gathered_scales[:, h * HALF:(h + 1) * HALF], start=True, stop=True)
+                banks.append(bank[:].rearrange("p (g j) -> p j g", j=PAGE))
+            return banks
+
+        a = product(k_words, ks, q_codes, q_scales, "a")
+        floors = shared.tile([P, G], F32, name="floors", offset=floors_at)
+        nc.vector.tensor_copy(floors[:], table[:].indirect(pages[:]))
+
+        neg_x = keep.tile([P, HALVES, PAGE, PAGES_H], F32, name="neg_x")
+        tau = keep.tile([P, HALVES, PAGE, PAGES_H], F32, name="tau")
+        sig = keep.tile([P, PAGE, HALVES, PAGES_H], F32, name="sig")
+        for h in range(HALVES):
+            floor_h = floors[:, h * PAGES_H:(h + 1) * PAGES_H].unsqueeze(1).to_broadcast([P, PAGE, PAGES_H])
+            nc.vector.scalar_tensor_tensor(out=neg_x[:, h], in0=floor_h, scalar=lam_sb[:], in1=a[h],
+                                           op0=ALU.mult, op1=ALU.subtract)
+            nc.scalar.activation(out=tau[:, h], in_=neg_x[:, h], func=ACT.Sigmoid)
+            nc.scalar.activation(out=sig[:, :, h, :], in_=neg_x[:, h], func=ACT.Sigmoid, scale=-1.0)
+        log_tau = keep.tile([P, I], F32, name="log_tau")
+        nc.scalar.activation(out=log_tau[:], in_=tau[:].rearrange("p h j g -> p (h j g)"), func=ACT.Ln,
+                             bias=LOG_FLOOR)
+
+        g_codes, g_scales = quantize(g_bf, "g")
+        vs = shared.tile([P, I], U8, name="vs", offset=floors_at, align_bytes=64)
+        nc.vector.tensor_copy(vs[:], v_scales[:].indirect(slots[:]))
+        c = product(v_words, vs, g_codes, g_scales, "c")
+
+        def page_sums(values, name):
+            flat = values[:].rearrange("p j h g -> p (j h g)")
+            turned = psum.tile([P, P], F32, name=name + "_turned")
+            steps = I // P
+            for s in range(steps):
+                nc.tensor.matmul(turned[:], lhsT=flat[:, s * P:(s + 1) * P], rhs=ident[:], is_transpose=True,
+                                 start=(s == 0), stop=(s == steps - 1))
+            turned_sb = keep.tile([P, P], F32, name=name + "_turned_sb")
+            nc.scalar.copy(out=turned_sb[:], in_=turned[:])
+            back = psum.tile([P, P], F32, name=name + "_back")
+            nc.tensor.transpose(back[:], turned_sb[:], ident[:])
+            return back
+
+        sig_sums = keep.tile([P, P], F32, name="sig_sums")
+        nc.scalar.activation(out=sig_sums[:], in_=page_sums(sig, "b")[:], func=ACT.Copy, scale=factor[:])
+
+        sig_c = keep.tile([P, PAGE, HALVES, PAGES_H], F32, name="sig_c")
+        for h in range(HALVES):
+            nc.vector.scalar_tensor_tensor(out=sig_c[:, :, h, :], in0=sig[:, :, h, :], scalar=factor[:], in1=c[h],
+                                           op0=ALU.mult, op1=ALU.mult)
+        sig_c_back = page_sums(sig_c, "a")
+
+        neg_p = keep.tile([P, HALVES, PAGE, PAGES_H], F32, name="neg_p")
+        neg_sum = keep.tile([P, 1], F32, name="neg_sum")
+        nc.vector.scalar_tensor_tensor(out=neg_p[:].rearrange("p h j g -> p (h j g)"), in0=log_tau[:], scalar=1.0,
+                                       in1=neg_x[:].rearrange("p h j g -> p (h j g)"), op0=ALU.mult, op1=ALU.min,
+                                       accum_out=neg_sum[:])
+        z = keep.tile([P, 1], F32, name="z")
+        nc.scalar.activation(out=z[:], in_=neg_sum[:], func=ACT.Identity, scale=-1.0, bias=res_sb[:])
+
+        neg_pc = keep.tile([P, HALVES, PAGE, PAGES_H], F32, name="neg_pc")
+        neg_dot = [keep.tile([P, 1], F32, name="neg_dot%d" % h) for h in range(HALVES)]
+        inv_z = keep.tile([P, 1], F32, name="inv_z")
+
+        def dot_half(h):
+            nc.vector.scalar_tensor_tensor(out=neg_pc[:, h], in0=neg_p[:, h], scalar=1.0, in1=c[h],
+                                           op0=ALU.mult, op1=ALU.mult, accum_out=neg_dot[h][:])
+
+        dot_half(0)
+        nc.vector.reciprocal(out=inv_z[:], in_=z[:])
+        dot_half(1)
+        inv_z2 = keep.tile([P, 1], F32, name="inv_z2")
+        nc.scalar.activation(out=inv_z2[:], in_=inv_z[:], func=ACT.Square)
+        direct = keep.tile([P, P], F32, name="direct")
+        nc.scalar.activation(out=direct[:], in_=sig_c_back[:], func=ACT.Copy, scale=inv_z[:])
+
+        dz = keep.tile([P, 1], F32, name="dz")
+        nc.vector.tensor_scalar(out=dz[:], in0=neg_dot[0][:], scalar1=neg_dot[1][:], scalar2=inv_z2[:],
+                                op0=ALU.add, op1=ALU.mult)
+        parts = keep.tile([P, P], F32, name="parts")
+        nc.vector.scalar_tensor_tensor(out=parts[:], in0=sig_sums[:], scalar=dz[:], in1=direct[:],
+                                       op0=ALU.mult, op1=ALU.add)
+        nc.vector.tensor_tensor(grad[:].indirect(pages[:]), parts[:, :G], parts[:, G:], ALU.add)
+
+        for h, queue in enumerate((nc.sync, nc.scalar)):
+            cols = slice(h * U // 2, (h + 1) * U // 2)
+            result = keep.tile([P, U // 2], F32, name="result%d" % h)
+            nc.vector.tensor_tensor(result[:], old_sb[:, cols], grad[:, cols], ALU.add)
+            queue.dma_start(out=out[:, cols], in_=result[:])

@@ -37,33 +37,37 @@ def tile_attend_bpagefloor_kernel(tc, query, keys_words, keys_scales, ptab, rese
         slots = lists.tile([P, I // 16], U16, name="slots")
         pages = lists.tile([P, G // 16], U16, name="pages")
 
-        ones_at = 8192
+        kscales_at = 0
+        kwords_at = 4096
         qraw_at = 16384
         qbf_at = 32768
-        floors_at = 40960
-        k_scales = keep.tile([P, T], U8, name="k_scales")
+        k_scales = shared.tile([P, T], U8, name="k_scales", offset=kscales_at)
         nc.vector.memset(k_scales[:].bitcast(I32), 0)
-        ones = shared.tile([P, P], F32, name="ones", offset=ones_at)
+        ones = keep.tile([P, P], F32, name="ones")
         nc.vector.memset(ones[:], 1.0)
         ident = keep.tile([P, P], F32, name="ident")
         nc.gpsimd.affine_select(out=ident[:], in_=ones[:], compare_op=ALU.is_equal, fill=0.0, base=0,
                                 pattern=[[-1, P]], channel_multiplier=1)
-        v_scales = shared.tile([P, T], U8, name="v_scales", offset=ones_at + 480)
+        v_scales = keep.tile([P, T], U8, name="v_scales")
         nc.vector.memset(v_scales[:].bitcast(I32), 0)
+        planes = keep.tile([P, 2 * I], U8, name="planes", align_bytes=64)
+        nc.vector.memset(planes[:].bitcast(I32), 0)
         grad = keep.tile([P, U], F32, name="grad")
         nc.vector.memset(grad[:], 0.0)
 
-        def load_scales(tile, scales):
-            rows = scales[0].rearrange("(quad r) c -> r quad c", r=4)
+        def load_scales(queue, tile, scales):
+            queue.dma_start(out=tile[32:96:4, :].bitcast(I32), in_=scales[0].bitcast(I32))
+
+        def place_scales(queue, plane, gathered):
             for r in range(4):
-                nc.sync.dma_start(out=tile[r:P:32, :].bitcast(I32), in_=rows[r].bitcast(I32))
+                queue.dma_start(out=plane[r:P:32, :].bitcast(I32), in_=gathered[32 + 4 * r:96:16, :].bitcast(I32))
 
         def interleave(raw, grouped):
             nc.scalar.copy(out=grouped[:].rearrange("p (c i) t -> p c t i", i=4),
                            in_=raw[:].rearrange("p t (c i) -> p c t i", i=4))
 
-        def quantize(grouped, name):
-            codes = keep.tile([P, Q], U32, name=name + "_codes", align_bytes=64)
+        def quantize(grouped, name, at):
+            codes = shared.tile([P, Q], U32, name=name + "_codes", align_bytes=64, offset=at)
             scales = keep.tile([P, Q], U8, name=name + "_scales", align_bytes=64)
             nc.vector.quantize_mx(out=codes[:].bitcast(FP8X4), scales=scales[:],
                                   in_=grouped[:].rearrange("p w t -> p (w t)"))
@@ -72,29 +76,30 @@ def tile_attend_bpagefloor_kernel(tc, query, keys_words, keys_scales, ptab, rese
         nc.sync.dma_start(slots[:], offs)
         q_raw = shared.tile([P, PACK, Q], F32, name="q_raw", offset=qraw_at)
         nc.sync.dma_start(out=q_raw[:], in_=query.rearrange("(p t) w -> p t w", t=PACK))
-        nc.sync.dma_start(pages[:], offs2)
-        load_scales(k_scales, keys_scales)
-        k_words = shared.tile([P, T], U16, name="k_words", offset=ones_at + 32 - 2 * T)
+        k_words = shared.tile([P, T], U16, name="k_words", offset=kwords_at)
         nc.sync.dma_start(out=k_words[:].bitcast(I32), in_=keys_words[0].bitcast(I32))
+        nc.sync.dma_start(pages[:], offs2)
+        load_scales(nc.scalar, k_scales, keys_scales)
+        load_scales(nc.sync, v_scales, vals_scales)
 
         q_bf = shared.tile([P, Q, PACK], BF16, name="q_bf", offset=qbf_at, align_bytes=64)
         interleave(q_raw, q_bf)
 
         table = shared.tile([P, U], F32, name="table", offset=qraw_at + 2016)
         nc.sync.dma_start(out=table[:], in_=ptab)
-        lam_sb = shared.tile([P, 1], F32, name="lam_sb", offset=ones_at + 64)
+        lam_sb = shared.tile([P, 1], F32, name="lam_sb", offset=qraw_at + 64)
         nc.sync.dma_start(out=lam_sb[:], in_=lam)
         g_raw = shared.tile([P, PACK, Q], F32, name="g_raw", offset=qraw_at + 32 - 2048)
         nc.sync.dma_start(out=g_raw[:], in_=gout.rearrange("(p t) w -> p t w", t=PACK))
-        load_scales(v_scales, vals_scales)
 
         ks = keep.tile([P, I], U8, name="ks", align_bytes=64)
         nc.vector.tensor_copy(ks[:], k_scales[:].indirect(slots[:]))
-        q_codes, q_scales = quantize(q_bf, "q")
+        place_scales(nc.scalar, planes[:, :I], ks)
+        q_codes, q_scales = quantize(q_bf, "q", kscales_at)
 
         v_words = shared.tile([P, T], U16, name="v_words", offset=qbf_at + 32 - 2 * T)
         nc.sync.dma_start(out=v_words[:].bitcast(I32), in_=vals_words[0].bitcast(I32))
-        res_sb = shared.tile([P, 1], F32, name="res_sb", offset=ones_at + 96)
+        res_sb = shared.tile([P, 1], F32, name="res_sb", offset=qraw_at + 96)
         nc.sync.dma_start(out=res_sb[:], in_=reserve)
         old_sb = shared.tile([P, U], F32, name="old_sb", offset=qbf_at + 992)
         nc.sync.dma_start(out=old_sb[:], in_=old)
@@ -117,13 +122,13 @@ def tile_attend_bpagefloor_kernel(tc, query, keys_words, keys_scales, ptab, rese
                 banks.append(bank[:].rearrange("p (g j) -> p j g", j=PAGE))
             return banks
 
-        a = product(k_words, ks, q_codes, q_scales, "a")
-        floors = shared.tile([P, G], F32, name="floors", offset=floors_at)
+        a = product(k_words, planes[:, :I], q_codes, q_scales, "a")
+        floors = shared.tile([P, G], F32, name="floors", offset=kwords_at + 1024)
         nc.vector.tensor_copy(floors[:], table[:].indirect(pages[:]))
 
         neg_x = keep.tile([P, HALVES, PAGE, PAGES_H], F32, name="neg_x")
-        tau = keep.tile([P, HALVES, PAGE, PAGES_H], F32, name="tau")
-        sig = keep.tile([P, PAGE, HALVES, PAGES_H], F32, name="sig")
+        tau = shared.tile([P, HALVES, PAGE, PAGES_H], F32, name="tau", offset=qraw_at - 4096)
+        sig = keep.tile([P, PAGE, HALVES, PAGES_H], F32, name="sig", tag="sig")
         for h in range(HALVES):
             floor_h = floors[:, h * PAGES_H:(h + 1) * PAGES_H].unsqueeze(1).to_broadcast([P, PAGE, PAGES_H])
             nc.vector.scalar_tensor_tensor(out=neg_x[:, h], in0=floor_h, scalar=lam_sb[:], in1=a[h],
@@ -134,10 +139,11 @@ def tile_attend_bpagefloor_kernel(tc, query, keys_words, keys_scales, ptab, rese
         nc.scalar.activation(out=log_tau[:], in_=tau[:].rearrange("p h j g -> p (h j g)"), func=ACT.Ln,
                              bias=LOG_FLOOR)
 
-        g_codes, g_scales = quantize(g_bf, "g")
-        vs = shared.tile([P, I], U8, name="vs", offset=floors_at, align_bytes=64)
+        vs = shared.tile([P, I], U8, name="vs", offset=kwords_at + 64, align_bytes=64)
         nc.vector.tensor_copy(vs[:], v_scales[:].indirect(slots[:]))
-        c = product(v_words, vs, g_codes, g_scales, "c")
+        place_scales(nc.sync, planes[:, I:], vs)
+        g_codes, g_scales = quantize(g_bf, "g", kwords_at + 1024 + 192)
+        c = product(v_words, planes[:, I:], g_codes, g_scales, "c")
 
         def page_sums(values, name):
             flat = values[:].rearrange("p j h g -> p (j h g)")
@@ -161,7 +167,7 @@ def tile_attend_bpagefloor_kernel(tc, query, keys_words, keys_scales, ptab, rese
                                            op0=ALU.mult, op1=ALU.mult)
         sig_c_back = page_sums(sig_c, "a")
 
-        neg_p = keep.tile([P, HALVES, PAGE, PAGES_H], F32, name="neg_p")
+        neg_p = keep.tile([P, HALVES, PAGE, PAGES_H], F32, name="neg_p", tag="sig")
         neg_sum = keep.tile([P, 1], F32, name="neg_sum")
         nc.vector.scalar_tensor_tensor(out=neg_p[:].rearrange("p h j g -> p (h j g)"), in0=log_tau[:], scalar=1.0,
                                        in1=neg_x[:].rearrange("p h j g -> p (h j g)"), op0=ALU.mult, op1=ALU.min,

@@ -18,11 +18,22 @@ ACT = mybir.ActivationFunctionType
 
 P = 128
 PACK = 4
+GROUP = 16
+QUAD = 32
+PLANE_ROWS = 4
 PAGE = I // G
 HALF = 512
 HALVES = I // HALF
 PAGES_H = HALF // PAGE
+LINE = 4
+GRAD_SCALE = 64.0
 LOG_FLOOR = 2.0 ** -60
+
+K_WORDS_AT = 0
+K_SCALES_AT = 24576
+FLOORS_AT = 45056
+BLOCK = 32
+MX_ALIGN = 64
 
 
 def tile_attend_bpagefloor_kernel(tc, query, keys_words, keys_scales, ptab, reserve, gout, vals_words,
@@ -34,14 +45,10 @@ def tile_attend_bpagefloor_kernel(tc, query, keys_words, keys_scales, ptab, rese
         shared = ctx.enter_context(tc.tile_pool(name="shared", bufs=1))
         psum = ctx.enter_context(tc.psum_pool(name="psum", bufs=1))
 
-        slots = lists.tile([P, I // 16], U16, name="slots")
-        pages = lists.tile([P, G // 16], U16, name="pages")
+        slots = lists.tile([P, I // GROUP], U16, name="slots")
+        pages = lists.tile([P, G // GROUP], U16, name="pages")
 
-        kscales_at = 0
-        kwords_at = 4096
-        qraw_at = 16384
-        qbf_at = 32768
-        k_scales = shared.tile([P, T], U8, name="k_scales", offset=kscales_at)
+        k_scales = shared.tile([P, T], U8, name="k_scales", offset=K_SCALES_AT)
         nc.vector.memset(k_scales[:].bitcast(I32), 0)
         ones = keep.tile([P, P], F32, name="ones")
         nc.vector.memset(ones[:], 1.0)
@@ -50,146 +57,184 @@ def tile_attend_bpagefloor_kernel(tc, query, keys_words, keys_scales, ptab, rese
                                 pattern=[[-1, P]], channel_multiplier=1)
         v_scales = keep.tile([P, T], U8, name="v_scales")
         nc.vector.memset(v_scales[:].bitcast(I32), 0)
-        planes = keep.tile([P, 2 * I], U8, name="planes", align_bytes=64)
-        nc.vector.memset(planes[:].bitcast(I32), 0)
+        k_plane = keep.tile([P, I], U8, name="k_plane", align_bytes=MX_ALIGN)
+        nc.vector.memset(k_plane[:].bitcast(I32), 0)
+        zeros = keep.tile([P, P], F32, name="zeros")
+        nc.vector.memset(zeros[:], 0.0)
         grad = keep.tile([P, U], F32, name="grad")
         nc.vector.memset(grad[:], 0.0)
 
-        def load_scales(queue, tile, scales):
-            queue.dma_start(out=tile[32:96:4, :].bitcast(I32), in_=scales[0].bitcast(I32))
+        nc.sync.dma_start(slots[:], offs)
+        nc.sync.dma_start(pages[:], offs2)
+        table = keep.tile([P, U], F32, name="table")
+        nc.sync.dma_start(out=table[:], in_=ptab)
+        nc.sync.dma_start(out=k_scales[QUAD:3 * QUAD:PLANE_ROWS, :].bitcast(I32), in_=keys_scales[0].bitcast(I32))
+        k_words = shared.tile([P, T], U16, name="k_words", offset=K_WORDS_AT)
+        nc.sync.dma_start(out=k_words[:].bitcast(I32), in_=keys_words[0].bitcast(I32))
+        q_raw = keep.tile([P, PACK, Q], F32, name="q_raw")
+        nc.sync.dma_start(out=q_raw[:], in_=query.rearrange("(p t) w -> p t w", t=PACK))
+        g_raw = keep.tile([P, PACK, Q], F32, name="g_raw")
+        nc.sync.dma_start(out=g_raw[:], in_=gout.rearrange("(p t) w -> p t w", t=PACK))
+        lam_sb = keep.tile([P, 1], F32, name="lam_sb")
+        nc.sync.dma_start(out=lam_sb[:], in_=lam)
+        v_rows = vals_scales[0].rearrange("(quad r) c -> r quad c", r=PLANE_ROWS)
+        for r in range(PLANE_ROWS):
+            nc.sync.dma_start(out=v_scales[r:P:QUAD, :].bitcast(I32), in_=v_rows[r].bitcast(I32))
 
-        def place_scales(queue, plane, gathered):
-            for r in range(4):
-                queue.dma_start(out=plane[r:P:32, :].bitcast(I32), in_=gathered[32 + 4 * r:96:16, :].bitcast(I32))
+        q_bf = keep.tile([P, Q, PACK], BF16, name="q_bf", align_bytes=MX_ALIGN)
+        g_bf = keep.tile([P, Q, PACK], BF16, name="g_bf", align_bytes=MX_ALIGN)
+        for raw, grouped in ((q_raw, q_bf), (g_raw, g_bf)):
+            nc.scalar.copy(out=grouped[:].rearrange("p (c i) t -> p c t i", i=LINE),
+                           in_=raw[:].rearrange("p t (c i) -> p c t i", i=LINE))
 
-        def interleave(raw, grouped):
-            nc.scalar.copy(out=grouped[:].rearrange("p (c i) t -> p c t i", i=4),
-                           in_=raw[:].rearrange("p t (c i) -> p c t i", i=4))
-
-        def quantize(grouped, name, at):
-            codes = shared.tile([P, Q], U32, name=name + "_codes", align_bytes=64, offset=at)
-            scales = keep.tile([P, Q], U8, name=name + "_scales", align_bytes=64)
+        def quantize(grouped, codes, name):
+            scales = keep.tile([P, Q], U8, name=name, align_bytes=MX_ALIGN)
             nc.vector.quantize_mx(out=codes[:].bitcast(FP8X4), scales=scales[:],
                                   in_=grouped[:].rearrange("p w t -> p (w t)"))
             return codes, scales
 
-        nc.sync.dma_start(slots[:], offs)
-        q_raw = shared.tile([P, PACK, Q], F32, name="q_raw", offset=qraw_at)
-        nc.sync.dma_start(out=q_raw[:], in_=query.rearrange("(p t) w -> p t w", t=PACK))
-        k_words = shared.tile([P, T], U16, name="k_words", offset=kwords_at)
-        nc.sync.dma_start(out=k_words[:].bitcast(I32), in_=keys_words[0].bitcast(I32))
-        nc.sync.dma_start(pages[:], offs2)
-        load_scales(nc.scalar, k_scales, keys_scales)
-        load_scales(nc.sync, v_scales, vals_scales)
-
-        q_bf = shared.tile([P, Q, PACK], BF16, name="q_bf", offset=qbf_at, align_bytes=64)
-        interleave(q_raw, q_bf)
-
-        table = shared.tile([P, U], F32, name="table", offset=qraw_at + 2016)
-        nc.sync.dma_start(out=table[:], in_=ptab)
-        lam_sb = shared.tile([P, 1], F32, name="lam_sb", offset=qraw_at + 64)
-        nc.sync.dma_start(out=lam_sb[:], in_=lam)
-        g_raw = shared.tile([P, PACK, Q], F32, name="g_raw", offset=qraw_at + 32 - 2048)
-        nc.sync.dma_start(out=g_raw[:], in_=gout.rearrange("(p t) w -> p t w", t=PACK))
-
-        ks = keep.tile([P, I], U8, name="ks", align_bytes=64)
-        nc.vector.tensor_copy(ks[:], k_scales[:].indirect(slots[:]))
-        place_scales(nc.scalar, planes[:, :I], ks)
-        q_codes, q_scales = quantize(q_bf, "q", kscales_at)
-
-        v_words = shared.tile([P, T], U16, name="v_words", offset=qbf_at + 32 - 2 * T)
-        nc.sync.dma_start(out=v_words[:].bitcast(I32), in_=vals_words[0].bitcast(I32))
-        res_sb = shared.tile([P, 1], F32, name="res_sb", offset=qraw_at + 96)
-        nc.sync.dma_start(out=res_sb[:], in_=reserve)
-        old_sb = shared.tile([P, U], F32, name="old_sb", offset=qbf_at + 992)
-        nc.sync.dma_start(out=old_sb[:], in_=old)
-
-        g_bf = keep.tile([P, Q, PACK], BF16, name="g_bf", align_bytes=64)
-        interleave(g_raw, g_bf)
         factor = keep.tile([P, 1], F32, name="factor")
-        nc.scalar.activation(out=factor[:], in_=lam_sb[:], func=ACT.Copy, scale=-64.0)
+        nc.scalar.activation(out=factor[:], in_=lam_sb[:], func=ACT.Copy, scale=-GRAD_SCALE)
 
-        def product(words, gathered_scales, codes, scales, name):
-            banks = []
-            for h in range(HALVES):
-                picked = keep.tile([P, HALF], U16, name="%s_picked%d" % (name, h), align_bytes=64)
-                cols = slice(h * HALF // 16, (h + 1) * HALF // 16)
-                nc.vector.tensor_copy(picked[:], words[:].indirect(slots[:, cols]))
-                bank = psum.tile([P, HALF], F32, name="%s_bank%d" % (name, h))
-                nc.tensor.matmul_mx(out=bank[:], lhsT=codes[:].bitcast(FP8X4), lhsT_scale=scales[:],
-                                    rhs=picked[:].bitcast(FP4X4),
-                                    rhs_scale=gathered_scales[:, h * HALF:(h + 1) * HALF], start=True, stop=True)
-                banks.append(bank[:].rearrange("p (g j) -> p j g", j=PAGE))
-            return banks
-
-        a = product(k_words, planes[:, :I], q_codes, q_scales, "a")
-        floors = shared.tile([P, G], F32, name="floors", offset=kwords_at + 1024)
+        floors = shared.tile([P, G], F32, name="floors", offset=FLOORS_AT)
         nc.vector.tensor_copy(floors[:], table[:].indirect(pages[:]))
+        ks = keep.tile([P, I], U8, name="ks")
+        nc.vector.tensor_copy(ks[:], k_scales[:].indirect(slots[:]))
+        for r in range(PLANE_ROWS):
+            rows = slice(QUAD + PLANE_ROWS * r, 3 * QUAD, PLANE_ROWS * PLANE_ROWS)
+            nc.sync.dma_start(out=k_plane[r:P:QUAD, :].bitcast(I32), in_=ks[rows, :].bitcast(I32))
+
+        res_sb = shared.tile([P, 1], F32, name="res_sb", offset=K_SCALES_AT + 2 * BLOCK)
+        nc.sync.dma_start(out=res_sb[:], in_=reserve)
+        old_sb = []
+        out_cols = [slice(0, U // 2), slice(U // 2, U)]
+        for n, cols in enumerate(out_cols):
+            old_part = shared.tile([P, U // 2], F32, name="old%d" % n, offset=K_SCALES_AT + 4 * BLOCK + n * 2 * U)
+            nc.sync.dma_start(out=old_part[:], in_=old[:, cols])
+            old_sb.append(old_part)
+        v_words = shared.tile([P, T], U16, name="v_words", offset=K_SCALES_AT + BLOCK - 2 * T)
+        nc.sync.dma_start(out=v_words[:].bitcast(I32), in_=vals_words[0].bitcast(I32))
+
+        def half_list(h):
+            return slots[:, h * HALF // GROUP:(h + 1) * HALF // GROUP]
+
+        def product(stationary, picked, plane, name):
+            codes, scales = stationary
+            bank = psum.tile([P, HALF], F32, name=name)
+            nc.tensor.matmul_mx(out=bank[:], lhsT=codes[:].bitcast(FP8X4), lhsT_scale=scales[:],
+                                rhs=picked[:].bitcast(FP4X4), rhs_scale=plane, start=True, stop=True)
+            return bank[:].rearrange("p (g j) -> p j g", j=PAGE)
+
+        k_picked = []
+        for h in range(HALVES):
+            picked = keep.tile([P, HALF], U16, name="k_picked%d" % h, tag="picked%d" % h, align_bytes=MX_ALIGN)
+            nc.vector.tensor_copy(picked[:], k_words[:].indirect(half_list(h)))
+            k_picked.append(picked)
+        q_codes = shared.tile([P, Q], U32, name="q_codes", align_bytes=MX_ALIGN, offset=K_WORDS_AT + HALF)
+        q_mx = quantize(q_bf, q_codes, "q_scales")
+        a = [product(q_mx, k_picked[h], k_plane[:, h * HALF:(h + 1) * HALF], "a%d" % h) for h in range(HALVES)]
+        vs0 = shared.tile([P, HALF], U8, name="vs0", offset=K_WORDS_AT, align_bytes=MX_ALIGN)
+        nc.vector.tensor_copy(vs0[:], v_scales[:].indirect(half_list(0)))
 
         neg_x = keep.tile([P, HALVES, PAGE, PAGES_H], F32, name="neg_x")
-        tau = shared.tile([P, HALVES, PAGE, PAGES_H], F32, name="tau", offset=qraw_at - 4096)
-        sig = keep.tile([P, PAGE, HALVES, PAGES_H], F32, name="sig", tag="sig")
+        tau = keep.tile([P, HALVES, PAGE, PAGES_H], F32, name="tau")
+        sig = keep.tile([P, PAGE, HALVES, PAGES_H], F32, name="sig")
         for h in range(HALVES):
             floor_h = floors[:, h * PAGES_H:(h + 1) * PAGES_H].unsqueeze(1).to_broadcast([P, PAGE, PAGES_H])
             nc.vector.scalar_tensor_tensor(out=neg_x[:, h], in0=floor_h, scalar=lam_sb[:], in1=a[h],
                                            op0=ALU.mult, op1=ALU.subtract)
-            nc.scalar.activation(out=tau[:, h], in_=neg_x[:, h], func=ACT.Sigmoid)
             nc.scalar.activation(out=sig[:, :, h, :], in_=neg_x[:, h], func=ACT.Sigmoid, scale=-1.0)
-        log_tau = keep.tile([P, I], F32, name="log_tau")
-        nc.scalar.activation(out=log_tau[:], in_=tau[:].rearrange("p h j g -> p (h j g)"), func=ACT.Ln,
-                             bias=LOG_FLOOR)
-
-        vs = shared.tile([P, I], U8, name="vs", offset=kwords_at + 64, align_bytes=64)
-        nc.vector.tensor_copy(vs[:], v_scales[:].indirect(slots[:]))
-        place_scales(nc.sync, planes[:, I:], vs)
-        g_codes, g_scales = quantize(g_bf, "g", kwords_at + 1024 + 192)
-        c = product(v_words, planes[:, I:], g_codes, g_scales, "c")
-
-        def page_sums(values, name):
-            flat = values[:].rearrange("p j h g -> p (j h g)")
-            turned = psum.tile([P, P], F32, name=name + "_turned")
-            steps = I // P
-            for s in range(steps):
-                nc.tensor.matmul(turned[:], lhsT=flat[:, s * P:(s + 1) * P], rhs=ident[:], is_transpose=True,
-                                 start=(s == 0), stop=(s == steps - 1))
-            turned_sb = keep.tile([P, P], F32, name=name + "_turned_sb")
-            nc.scalar.copy(out=turned_sb[:], in_=turned[:])
-            back = psum.tile([P, P], F32, name=name + "_back")
-            nc.tensor.transpose(back[:], turned_sb[:], ident[:])
-            return back
-
-        sig_sums = keep.tile([P, P], F32, name="sig_sums")
-        nc.scalar.activation(out=sig_sums[:], in_=page_sums(sig, "b")[:], func=ACT.Copy, scale=factor[:])
-
-        sig_c = keep.tile([P, PAGE, HALVES, PAGES_H], F32, name="sig_c")
+            nc.scalar.activation(out=tau[:, h], in_=neg_x[:, h], func=ACT.Sigmoid)
+        sig_c = keep.tile([P, HALVES, PAGE, PAGES_H], F32, name="sig_c")
+        log_tau1 = keep.tile([P, PAGE, PAGES_H], F32, name="log_tau1")
+        log_tau = [sig_c[:, 1], log_tau1[:]]
         for h in range(HALVES):
-            nc.vector.scalar_tensor_tensor(out=sig_c[:, :, h, :], in0=sig[:, :, h, :], scalar=factor[:], in1=c[h],
-                                           op0=ALU.mult, op1=ALU.mult)
-        sig_c_back = page_sums(sig_c, "a")
+            nc.scalar.activation(out=log_tau[h], in_=tau[:, h], func=ACT.Ln, bias=LOG_FLOOR)
 
-        neg_p = keep.tile([P, HALVES, PAGE, PAGES_H], F32, name="neg_p", tag="sig")
-        neg_sum = keep.tile([P, 1], F32, name="neg_sum")
-        nc.vector.scalar_tensor_tensor(out=neg_p[:].rearrange("p h j g -> p (h j g)"), in0=log_tau[:], scalar=1.0,
-                                       in1=neg_x[:].rearrange("p h j g -> p (h j g)"), op0=ALU.mult, op1=ALU.min,
-                                       accum_out=neg_sum[:])
-        z = keep.tile([P, 1], F32, name="z")
-        nc.scalar.activation(out=z[:], in_=neg_sum[:], func=ACT.Identity, scale=-1.0, bias=res_sb[:])
+        g_codes = keep.tile([P, Q], U32, name="g_codes", tag="picked0", align_bytes=MX_ALIGN)
+        g_mx = quantize(g_bf, g_codes, "g_scales")
 
-        neg_pc = keep.tile([P, HALVES, PAGE, PAGES_H], F32, name="neg_pc")
+        vs1 = shared.tile([P, HALF], U8, name="vs1", offset=FLOORS_AT + MX_ALIGN - HALF, align_bytes=MX_ALIGN)
+        nc.vector.tensor_copy(vs1[:], v_scales[:].indirect(half_list(1)))
+        v_picked0_at = FLOORS_AT + 4 * G - MX_ALIGN
+        v_picked0 = shared.tile([P, HALF], U16, name="v_picked0", offset=v_picked0_at, align_bytes=MX_ALIGN)
+        v_picked1 = keep.tile([P, HALF], U16, name="v_picked1", tag="picked1", align_bytes=MX_ALIGN)
+        c = []
+        for h, (picked, plane) in enumerate(((v_picked0, vs0), (v_picked1, vs1))):
+            nc.vector.tensor_copy(picked[:], v_words[:].indirect(half_list(h)))
+            c.append(product(g_mx, picked, plane[:], "c%d" % h))
+
+        def turn(out_ap, in_ap, start, stop):
+            nc.tensor.matmul(out_ap, lhsT=in_ap, rhs=ident[:], is_transpose=True, start=start, stop=stop)
+
+        def turned_sum(flat, name):
+            blocks = flat.shape[1] // P
+            turned = psum.tile([P, P], F32, name=name)
+            for s in range(blocks):
+                turn(turned[:], flat[:, s * P:(s + 1) * P], s == 0, s == blocks - 1)
+            turned_sb = keep.tile([P, P], F32, name=name + "_sb")
+            nc.scalar.copy(out=turned_sb[:], in_=turned[:])
+            return turned_sb
+
+        sig_turned = turned_sum(sig[:].rearrange("p j h g -> p (j h g)"), "sig_turned")
+        sig_back = psum.tile([P, P], F32, name="sig_back", tag="a0")
+        turn(sig_back[:], sig_turned[:], True, True)
+        sig_sums = keep.tile([P, P], F32, name="sig_sums")
+        nc.scalar.activation(out=sig_sums[:], in_=sig_back[:], func=ACT.Copy, scale=factor[:])
+
+        span = P + G
+        folded = psum.tile([P, HALVES, span], F32, name="folded")
+        folded_flat = folded[:].rearrange("p h w -> p (h w)")
+        for s in range(HALVES * span // P):
+            turn(folded_flat[:, s * P:(s + 1) * P], zeros[:], s == 0, False)
+
+        def fold(h):
+            turned = turned_sum(sig_c[:, h].rearrange("p j g -> p (j g)"), "sig_c_turned%d" % h)
+            turn(folded[:, h, :P], turned[:], False, False)
+            turn(folded[:, h, G:], turned[:], False, h == HALVES - 1)
+
+        neg_p = [shared.tile([P, PAGE, PAGES_H], F32, name="neg_p0", offset=v_picked0_at),
+                 keep.tile([P, PAGE, PAGES_H], F32, name="neg_p1", tag="picked1", align_bytes=MX_ALIGN)]
+        neg_sum = [keep.tile([P, 1], F32, name="neg_sum%d" % h) for h in range(HALVES)]
         neg_dot = [keep.tile([P, 1], F32, name="neg_dot%d" % h) for h in range(HALVES)]
-        inv_z = keep.tile([P, 1], F32, name="inv_z")
+        neg_pc = keep.tile([P, HALVES, PAGE, PAGES_H], F32, name="neg_pc")
+
+        def weigh(h, places):
+            nc.vector.scalar_tensor_tensor(out=sig_c[:, h, places, :], in0=sig[:, places, h, :], scalar=factor[:],
+                                           in1=c[h][:, places, :], op0=ALU.mult, op1=ALU.mult)
+
+        def softplus(h):
+            nc.vector.scalar_tensor_tensor(out=neg_p[h][:], in0=log_tau[h], scalar=1.0, in1=neg_x[:, h],
+                                           op0=ALU.mult, op1=ALU.min, accum_out=neg_sum[h][:])
 
         def dot_half(h):
-            nc.vector.scalar_tensor_tensor(out=neg_pc[:, h], in0=neg_p[:, h], scalar=1.0, in1=c[h],
+            nc.vector.scalar_tensor_tensor(out=neg_pc[:, h], in0=neg_p[h][:], scalar=1.0, in1=c[h],
                                            op0=ALU.mult, op1=ALU.mult, accum_out=neg_dot[h][:])
 
+        weigh(0, slice(0, PAGE))
+        softplus(0)
+        fold(0)
+        weigh(1, slice(0, PAGE // 2))
+        weigh(1, slice(PAGE // 2, PAGE))
+        softplus(1)
+        z_first = keep.tile([P, 1], F32, name="z_first")
+        nc.gpsimd.tensor_scalar(out=z_first[:], in0=neg_sum[0][:], scalar1=-1.0, scalar2=res_sb[:],
+                                op0=ALU.mult, op1=ALU.add)
+        z = keep.tile([P, 1], F32, name="z")
+        nc.gpsimd.tensor_scalar(out=z[:], in0=neg_sum[1][:], scalar1=-1.0, scalar2=z_first[:],
+                                op0=ALU.mult, op1=ALU.add)
+        fold(1)
+
+        inv_z = keep.tile([P, 1], F32, name="inv_z")
         dot_half(0)
         nc.vector.reciprocal(out=inv_z[:], in_=z[:])
         dot_half(1)
         inv_z2 = keep.tile([P, 1], F32, name="inv_z2")
-        nc.scalar.activation(out=inv_z2[:], in_=inv_z[:], func=ACT.Square)
+        nc.gpsimd.tensor_tensor(inv_z2[:], inv_z[:], inv_z[:], ALU.mult)
         direct = keep.tile([P, P], F32, name="direct")
-        nc.scalar.activation(out=direct[:], in_=sig_c_back[:], func=ACT.Copy, scale=inv_z[:])
+        nc.scalar.activation(out=direct[:].rearrange("p (e h g) -> p e h g", e=2, h=HALVES),
+                             in_=folded[:, :, G:P].rearrange("p h (e g) -> p e h g", e=2),
+                             func=ACT.Copy, scale=inv_z[:])
 
         dz = keep.tile([P, 1], F32, name="dz")
         nc.vector.tensor_scalar(out=dz[:], in0=neg_dot[0][:], scalar1=neg_dot[1][:], scalar2=inv_z2[:],
@@ -199,8 +244,7 @@ def tile_attend_bpagefloor_kernel(tc, query, keys_words, keys_scales, ptab, rese
                                        op0=ALU.mult, op1=ALU.add)
         nc.vector.tensor_tensor(grad[:].indirect(pages[:]), parts[:, :G], parts[:, G:], ALU.add)
 
-        for h, queue in enumerate((nc.sync, nc.scalar)):
-            cols = slice(h * U // 2, (h + 1) * U // 2)
-            result = keep.tile([P, U // 2], F32, name="result%d" % h)
-            nc.vector.tensor_tensor(result[:], old_sb[:, cols], grad[:, cols], ALU.add)
+        for n, (cols, queue) in enumerate(zip(out_cols, (nc.sync, nc.scalar))):
+            result = keep.tile([P, U // 2], F32, name="result%d" % n)
+            nc.vector.tensor_tensor(result[:], old_sb[n][:], grad[:, cols], ALU.add)
             queue.dma_start(out=out[:, cols], in_=result[:])

from contextlib import ExitStack

import concourse.mybir as mybir

D, T, I, G, U, Q = 512, 4096, 1024, 64, 512, 128
FLOPS = 2 * 2 * D * I * Q

F32 = mybir.dt.float32
BF16 = mybir.dt.bfloat16
I32 = mybir.dt.int32
U32 = mybir.dt.uint32
U16 = mybir.dt.uint16
U8 = mybir.dt.uint8
FP8X4 = mybir.dt.float8_e4m3fn_x4
FP4X4 = mybir.dt.float4_e2m1fn_x4
ALU = mybir.AluOpType
ACT = mybir.ActivationFunctionType

P = 128
PACK = 4
GROUP = 16
QUAD = 32
PLANE_ROWS = 4
PAGE = I // G
HALF = 512
HALVES = I // HALF
PAGES_H = HALF // PAGE
LINE = 4
GRAD_SCALE = 64.0
LOG_FLOOR = 2.0 ** -60

K_WORDS_AT = 0
K_SCALES_AT = 24576
FLOORS_AT = 45056
BLOCK = 32
MX_ALIGN = 64


def tile_attend_bpagefloor_kernel(tc, query, keys_words, keys_scales, ptab, reserve, gout, vals_words,
                                   vals_scales, lam, old, offs, offs2, out):
    nc = tc.nc
    with ExitStack() as ctx:
        lists = ctx.enter_context(tc.tile_pool(name="lists", bufs=1))
        keep = ctx.enter_context(tc.tile_pool(name="keep", bufs=1))
        shared = ctx.enter_context(tc.tile_pool(name="shared", bufs=1))
        psum = ctx.enter_context(tc.psum_pool(name="psum", bufs=1))

        slots = lists.tile([P, I // GROUP], U16, name="slots")
        pages = lists.tile([P, G // GROUP], U16, name="pages")

        k_scales = shared.tile([P, T], U8, name="k_scales", offset=K_SCALES_AT)
        nc.vector.memset(k_scales[:].bitcast(I32), 0)
        ones = keep.tile([P, P], F32, name="ones")
        nc.vector.memset(ones[:], 1.0)
        ident = keep.tile([P, P], F32, name="ident")
        nc.gpsimd.affine_select(out=ident[:], in_=ones[:], compare_op=ALU.is_equal, fill=0.0, base=0,
                                pattern=[[-1, P]], channel_multiplier=1)
        v_scales = keep.tile([P, T], U8, name="v_scales")
        nc.vector.memset(v_scales[:].bitcast(I32), 0)
        k_plane = keep.tile([P, I], U8, name="k_plane", align_bytes=MX_ALIGN)
        nc.vector.memset(k_plane[:].bitcast(I32), 0)
        zeros = keep.tile([P, P], F32, name="zeros")
        nc.vector.memset(zeros[:], 0.0)
        grad = keep.tile([P, U], F32, name="grad")
        nc.vector.memset(grad[:], 0.0)

        nc.sync.dma_start(slots[:], offs)
        nc.sync.dma_start(pages[:], offs2)
        table = keep.tile([P, U], F32, name="table")
        nc.sync.dma_start(out=table[:], in_=ptab)
        nc.sync.dma_start(out=k_scales[QUAD:3 * QUAD:PLANE_ROWS, :].bitcast(I32), in_=keys_scales[0].bitcast(I32))
        k_words = shared.tile([P, T], U16, name="k_words", offset=K_WORDS_AT)
        nc.sync.dma_start(out=k_words[:].bitcast(I32), in_=keys_words[0].bitcast(I32))
        q_raw = keep.tile([P, PACK, Q], F32, name="q_raw")
        nc.sync.dma_start(out=q_raw[:], in_=query.rearrange("(p t) w -> p t w", t=PACK))
        g_raw = keep.tile([P, PACK, Q], F32, name="g_raw")
        nc.sync.dma_start(out=g_raw[:], in_=gout.rearrange("(p t) w -> p t w", t=PACK))
        lam_sb = keep.tile([P, 1], F32, name="lam_sb")
        nc.sync.dma_start(out=lam_sb[:], in_=lam)
        v_rows = vals_scales[0].rearrange("(quad r) c -> r quad c", r=PLANE_ROWS)
        for r in range(PLANE_ROWS):
            nc.sync.dma_start(out=v_scales[r:P:QUAD, :].bitcast(I32), in_=v_rows[r].bitcast(I32))

        q_bf = keep.tile([P, Q, PACK], BF16, name="q_bf", align_bytes=MX_ALIGN)
        g_bf = keep.tile([P, Q, PACK], BF16, name="g_bf", align_bytes=MX_ALIGN)
        for raw, grouped in ((q_raw, q_bf), (g_raw, g_bf)):
            nc.scalar.copy(out=grouped[:].rearrange("p (c i) t -> p c t i", i=LINE),
                           in_=raw[:].rearrange("p t (c i) -> p c t i", i=LINE))

        def quantize(grouped, codes, name):
            scales = keep.tile([P, Q], U8, name=name, align_bytes=MX_ALIGN)
            nc.vector.quantize_mx(out=codes[:].bitcast(FP8X4), scales=scales[:],
                                  in_=grouped[:].rearrange("p w t -> p (w t)"))
            return codes, scales

        factor = keep.tile([P, 1], F32, name="factor")
        nc.scalar.activation(out=factor[:], in_=lam_sb[:], func=ACT.Copy, scale=-GRAD_SCALE)

        floors = shared.tile([P, G], F32, name="floors", offset=FLOORS_AT)
        nc.vector.tensor_copy(floors[:], table[:].indirect(pages[:]))
        ks = keep.tile([P, I], U8, name="ks")
        nc.vector.tensor_copy(ks[:], k_scales[:].indirect(slots[:]))
        for r in range(PLANE_ROWS):
            rows = slice(QUAD + PLANE_ROWS * r, 3 * QUAD, PLANE_ROWS * PLANE_ROWS)
            nc.sync.dma_start(out=k_plane[r:P:QUAD, :].bitcast(I32), in_=ks[rows, :].bitcast(I32))

        res_sb = shared.tile([P, 1], F32, name="res_sb", offset=K_SCALES_AT + 2 * BLOCK)
        nc.sync.dma_start(out=res_sb[:], in_=reserve)
        old_sb = []
        out_cols = [slice(0, U // 2), slice(U // 2, U)]
        for n, cols in enumerate(out_cols):
            old_part = shared.tile([P, U // 2], F32, name="old%d" % n, offset=K_SCALES_AT + 4 * BLOCK + n * 2 * U)
            nc.sync.dma_start(out=old_part[:], in_=old[:, cols])
            old_sb.append(old_part)
        v_words = shared.tile([P, T], U16, name="v_words", offset=K_SCALES_AT + BLOCK - 2 * T)
        nc.sync.dma_start(out=v_words[:].bitcast(I32), in_=vals_words[0].bitcast(I32))

        def half_list(h):
            return slots[:, h * HALF // GROUP:(h + 1) * HALF // GROUP]

        def product(stationary, picked, plane, name):
            codes, scales = stationary
            bank = psum.tile([P, HALF], F32, name=name)
            nc.tensor.matmul_mx(out=bank[:], lhsT=codes[:].bitcast(FP8X4), lhsT_scale=scales[:],
                                rhs=picked[:].bitcast(FP4X4), rhs_scale=plane, start=True, stop=True)
            return bank[:].rearrange("p (g j) -> p j g", j=PAGE)

        k_picked = []
        for h in range(HALVES):
            picked = keep.tile([P, HALF], U16, name="k_picked%d" % h, tag="picked%d" % h, align_bytes=MX_ALIGN)
            nc.vector.tensor_copy(picked[:], k_words[:].indirect(half_list(h)))
            k_picked.append(picked)
        q_codes = shared.tile([P, Q], U32, name="q_codes", align_bytes=MX_ALIGN, offset=K_WORDS_AT + HALF)
        q_mx = quantize(q_bf, q_codes, "q_scales")
        a = [product(q_mx, k_picked[h], k_plane[:, h * HALF:(h + 1) * HALF], "a%d" % h) for h in range(HALVES)]
        vs0 = shared.tile([P, HALF], U8, name="vs0", offset=K_WORDS_AT, align_bytes=MX_ALIGN)
        nc.vector.tensor_copy(vs0[:], v_scales[:].indirect(half_list(0)))

        neg_x = keep.tile([P, HALVES, PAGE, PAGES_H], F32, name="neg_x")
        tau = keep.tile([P, HALVES, PAGE, PAGES_H], F32, name="tau")
        sig = keep.tile([P, PAGE, HALVES, PAGES_H], F32, name="sig")
        for h in range(HALVES):
            floor_h = floors[:, h * PAGES_H:(h + 1) * PAGES_H].unsqueeze(1).to_broadcast([P, PAGE, PAGES_H])
            nc.vector.scalar_tensor_tensor(out=neg_x[:, h], in0=floor_h, scalar=lam_sb[:], in1=a[h],
                                           op0=ALU.mult, op1=ALU.subtract)
            nc.scalar.activation(out=sig[:, :, h, :], in_=neg_x[:, h], func=ACT.Sigmoid, scale=-1.0)
            nc.scalar.activation(out=tau[:, h], in_=neg_x[:, h], func=ACT.Sigmoid)
        sig_c = keep.tile([P, HALVES, PAGE, PAGES_H], F32, name="sig_c")
        log_tau1 = keep.tile([P, PAGE, PAGES_H], F32, name="log_tau1")
        log_tau = [sig_c[:, 1], log_tau1[:]]
        for h in range(HALVES):
            nc.scalar.activation(out=log_tau[h], in_=tau[:, h], func=ACT.Ln, bias=LOG_FLOOR)

        g_codes = keep.tile([P, Q], U32, name="g_codes", tag="picked0", align_bytes=MX_ALIGN)
        g_mx = quantize(g_bf, g_codes, "g_scales")

        vs1 = shared.tile([P, HALF], U8, name="vs1", offset=FLOORS_AT + MX_ALIGN - HALF, align_bytes=MX_ALIGN)
        nc.vector.tensor_copy(vs1[:], v_scales[:].indirect(half_list(1)))
        v_picked0_at = FLOORS_AT + 4 * G - MX_ALIGN
        v_picked0 = shared.tile([P, HALF], U16, name="v_picked0", offset=v_picked0_at, align_bytes=MX_ALIGN)
        v_picked1 = keep.tile([P, HALF], U16, name="v_picked1", tag="picked1", align_bytes=MX_ALIGN)
        c = []
        for h, (picked, plane) in enumerate(((v_picked0, vs0), (v_picked1, vs1))):
            nc.vector.tensor_copy(picked[:], v_words[:].indirect(half_list(h)))
            c.append(product(g_mx, picked, plane[:], "c%d" % h))

        def turn(out_ap, in_ap, start, stop):
            nc.tensor.matmul(out_ap, lhsT=in_ap, rhs=ident[:], is_transpose=True, start=start, stop=stop)

        def turned_sum(flat, name):
            blocks = flat.shape[1] // P
            turned = psum.tile([P, P], F32, name=name)
            for s in range(blocks):
                turn(turned[:], flat[:, s * P:(s + 1) * P], s == 0, s == blocks - 1)
            turned_sb = keep.tile([P, P], F32, name=name + "_sb")
            nc.scalar.copy(out=turned_sb[:], in_=turned[:])
            return turned_sb

        sig_turned = turned_sum(sig[:].rearrange("p j h g -> p (j h g)"), "sig_turned")
        sig_back = psum.tile([P, P], F32, name="sig_back", tag="a0")
        turn(sig_back[:], sig_turned[:], True, True)
        sig_sums = keep.tile([P, P], F32, name="sig_sums")
        nc.scalar.activation(out=sig_sums[:], in_=sig_back[:], func=ACT.Copy, scale=factor[:])

        span = P + G
        folded = psum.tile([P, HALVES, span], F32, name="folded")
        folded_flat = folded[:].rearrange("p h w -> p (h w)")
        for s in range(HALVES * span // P):
            turn(folded_flat[:, s * P:(s + 1) * P], zeros[:], s == 0, False)

        def fold(h):
            turned = turned_sum(sig_c[:, h].rearrange("p j g -> p (j g)"), "sig_c_turned%d" % h)
            turn(folded[:, h, :P], turned[:], False, False)
            turn(folded[:, h, G:], turned[:], False, h == HALVES - 1)

        neg_p = [shared.tile([P, PAGE, PAGES_H], F32, name="neg_p0", offset=v_picked0_at),
                 keep.tile([P, PAGE, PAGES_H], F32, name="neg_p1", tag="picked1", align_bytes=MX_ALIGN)]
        neg_sum = [keep.tile([P, 1], F32, name="neg_sum%d" % h) for h in range(HALVES)]
        neg_dot = [keep.tile([P, 1], F32, name="neg_dot%d" % h) for h in range(HALVES)]
        neg_pc = keep.tile([P, HALVES, PAGE, PAGES_H], F32, name="neg_pc")

        def weigh(h, places):
            nc.vector.scalar_tensor_tensor(out=sig_c[:, h, places, :], in0=sig[:, places, h, :], scalar=factor[:],
                                           in1=c[h][:, places, :], op0=ALU.mult, op1=ALU.mult)

        def softplus(h):
            nc.vector.scalar_tensor_tensor(out=neg_p[h][:], in0=log_tau[h], scalar=1.0, in1=neg_x[:, h],
                                           op0=ALU.mult, op1=ALU.min, accum_out=neg_sum[h][:])

        def dot_half(h):
            nc.vector.scalar_tensor_tensor(out=neg_pc[:, h], in0=neg_p[h][:], scalar=1.0, in1=c[h],
                                           op0=ALU.mult, op1=ALU.mult, accum_out=neg_dot[h][:])

        weigh(0, slice(0, PAGE))
        softplus(0)
        fold(0)
        weigh(1, slice(0, PAGE // 2))
        weigh(1, slice(PAGE // 2, PAGE))
        softplus(1)
        z_first = keep.tile([P, 1], F32, name="z_first")
        nc.gpsimd.tensor_scalar(out=z_first[:], in0=neg_sum[0][:], scalar1=-1.0, scalar2=res_sb[:],
                                op0=ALU.mult, op1=ALU.add)
        z = keep.tile([P, 1], F32, name="z")
        nc.gpsimd.tensor_scalar(out=z[:], in0=neg_sum[1][:], scalar1=-1.0, scalar2=z_first[:],
                                op0=ALU.mult, op1=ALU.add)
        fold(1)

        inv_z = keep.tile([P, 1], F32, name="inv_z")
        dot_half(0)
        nc.vector.reciprocal(out=inv_z[:], in_=z[:])
        dot_half(1)
        inv_z2 = keep.tile([P, 1], F32, name="inv_z2")
        nc.gpsimd.tensor_tensor(inv_z2[:], inv_z[:], inv_z[:], ALU.mult)
        direct = keep.tile([P, P], F32, name="direct")
        nc.scalar.activation(out=direct[:].rearrange("p (e h g) -> p e h g", e=2, h=HALVES),
                             in_=folded[:, :, G:P].rearrange("p h (e g) -> p e h g", e=2),
                             func=ACT.Copy, scale=inv_z[:])

        dz = keep.tile([P, 1], F32, name="dz")
        nc.vector.tensor_scalar(out=dz[:], in0=neg_dot[0][:], scalar1=neg_dot[1][:], scalar2=inv_z2[:],
                                op0=ALU.add, op1=ALU.mult)
        parts = keep.tile([P, P], F32, name="parts")
        nc.vector.scalar_tensor_tensor(out=parts[:], in0=sig_sums[:], scalar=dz[:], in1=direct[:],
                                       op0=ALU.mult, op1=ALU.add)
        nc.vector.tensor_tensor(grad[:].indirect(pages[:]), parts[:, :G], parts[:, G:], ALU.add)

        for n, (cols, queue) in enumerate(zip(out_cols, (nc.sync, nc.scalar))):
            result = keep.tile([P, U // 2], F32, name="result%d" % n)
            nc.vector.tensor_tensor(result[:], old_sb[n][:], grad[:, cols], ALU.add)
            queue.dma_start(out=out[:, cols], in_=result[:])
